import numpy as np, ml_dtypes
CORES = [3,7,11,15,131,135,139,143]
N = 8
import mx_ref
BF = ml_dtypes.bfloat16
def entries(a):
    return np.ascontiguousarray(a.T).reshape(-1)
def table(e):
    return np.ascontiguousarray(np.reshape(e, (-1, 16)).T).astype(np.int32)
def cols(t, e):
    v = np.concatenate([t.reshape(128, -1, 4), np.zeros((128, 1, 4), BF)], axis=1)
    return np.ascontiguousarray(v[:, e]).reshape(128, -1)
def cut(t, i, w=512):
    return t[:, w * i:w * i + w]
def f(rng, *shape):
    return mx_ref.flush((rng.standard_normal(shape, dtype=np.float32) * np.exp2(rng.integers(-2, 3, shape[:-1] + (1,)))).astype(BF))
def wide(rng, *shape, cols=0):
    v = rng.standard_normal(shape, dtype=np.float32) * np.exp2(rng.integers(-12, 13, shape)).astype(np.float32)
    if cols: v *= np.repeat(np.exp2(rng.integers(-cols, cols + 1, shape[:-2] + (1, shape[-1] // 4))) * (rng.random(shape[:-2] + (1, shape[-1] // 4)) > 0.0625), 4, axis=-1).astype(np.float32)
    return mx_ref.flush(v.astype(BF))
T, CAPP, F = 128, 80, 8
def inverse(e):
    o = np.full(F * T, -1)
    k = np.flatnonzero(e >= 0); k = k[np.argsort(e[k], kind="stable")]; v = e[k]
    at = np.arange(len(k)) - np.searchsorted(v, v); keep = at < F
    o[(F * v + at)[keep]] = k[keep]
    return o
def counts(rng, most=CAPP):
    n = np.zeros((N, N), int)
    for r in range(N):
        a = rng.integers(T // N, 4 * T // N + 1, N)
        n[:, r] = a + np.bincount(rng.permutation(np.repeat(np.arange(N), most - a))[:4 * T - a.sum()], minlength=N)
    return n
def senders(rng, n):
    return np.stack([rng.permutation(np.repeat(np.arange(N), n[:, r])) for r in range(N)])
def lists(rng, A, node=None, top=None, popular=False, big=None):
    sn = np.full((N, N * CAPP), -1); nb = np.zeros((N, 4 * T), int)
    for s in range(N):
        d, e = np.nonzero(A == s); free = rng.permutation(T)
        if node is not None: v = node[d, e]
        elif top is not None:
            t = top[d, e]; h = (t.sum() + F - 1) // F; v = np.zeros(len(d), int); big.append(free[:h])
            v[t] = rng.permutation(np.repeat(free[:h], F))[:t.sum()]
            v[~t] = rng.permutation(np.repeat(free[h:], F))[:(~t).sum()]
        else:
            h = len(d) // 16 if popular else 0
            v = rng.permutation(np.concatenate([np.repeat(free[:h], F), rng.permutation(np.repeat(free[h:], F))[:len(d) - F * h]]))
        for q in range(N):
            k = np.flatnonzero(d == q); c = rng.permutation(CAPP)[:len(k)]
            sn[s, q * CAPP + c] = v[k]; nb[q, e[k]] = s * CAPP + c
    return {"sn": np.stack([table(a) for a in sn]), "nb": np.stack([table(a) for a in nb]), "il": np.stack([table(inverse(a)) for a in sn])}
def setup_inputs(rng):
    return {"x": f(rng, N, 128, 4 * T), "gr": f(rng, N, 128, 4 * T), "w": np.repeat(f(rng, 1, 128, 2048), N, axis=0), "w2": np.repeat(f(rng, 1, 128, 2048), N, axis=0), **lists(rng, senders(rng, counts(rng)))}
def setup_inputs_ties(rng):
    d = setup_inputs(rng); own = d["x"].reshape(N, 128, T, 4)
    d["x"] = np.ascontiguousarray(np.where(rng.random((N, 1, T, 1)) < 0.7, own[:1], own)).reshape(N, 128, 4 * T)
    n = counts(rng, min(CAPP, T)); A = np.zeros((N, 4 * T), int); node = np.zeros((N, 4 * T), int)
    e = np.arange(4 * T); j = e % T; k = (e // T + j) % 4
    for r in range(N):
        o = rng.permutation(N); to = 4 * rng.permutation(T)[j] + k
        A[r, to] = np.repeat(o, n[o, r]); node[r, to] = rng.permutation(T)[j]
    return {**d, **lists(rng, A, node=node)}
def setup_inputs_oneside(rng):
    d = setup_inputs(rng); top = np.zeros((N, 4 * T), bool); big = []
    for r in range(N): top[r, 4 * rng.permutation(T)[:T // 2] + 3] = True
    d.update(lists(rng, senders(rng, counts(rng)), top=top, big=big))
    v = np.abs(d["x"].astype(np.float32)).reshape(N, 128, T, 4)
    for s in range(N): v[s][:, big[s]] *= 64
    d["x"] = v.reshape(N, 128, 4 * T).astype(BF); d["w"] = np.abs(d["w"].astype(np.float32)).astype(BF)
    return d
def setup_inputs_popular(rng):
    return {**setup_inputs(rng), **lists(rng, senders(rng, counts(rng)), popular=True)}
def setup_inputs_full(rng):
    n = np.zeros((N, N), int); o = rng.permutation(N); at = rng.permutation(N)
    m = 4 * T // CAPP; rest = 4 * T - m * CAPP
    for r in range(N):
        for j in range(m): n[o[(at[r] + j) % N], r] = CAPP
        if rest: n[o[(at[r] + m) % N], r] = rest
    return {**setup_inputs(rng), **lists(rng, senders(rng, n))}
def setup_inputs_spread(rng):
    d = setup_inputs(rng); d["x"] = wide(rng, N, 128, 4 * T, cols=8); return d
def check_inputs(d):
    b = []
    for t in ("w", "w2"):
        if (d[t] != d[t][:1]).any(): b.append(t)
    e = np.stack([entries(a) for a in d["sn"]])
    if e.min() < -1 or e.max() >= T: b.append("sn")
    e = np.clip(e, -1, T - 1)
    for r in range(N):
        if np.bincount(e[r][e[r] >= 0], minlength=T).max() > F: b.append("sn")
        if not np.array_equal(np.sort(entries(d["nb"][r])), np.flatnonzero(e[:, r * CAPP:(r + 1) * CAPP].reshape(-1) >= 0)): b.append("nb")
        if not np.array_equal(entries(d["il"][r]), inverse(e[r])): b.append("il")
    return b
def four(v):
    return [mx_ref.quantize(np.ascontiguousarray(cut(v, b))) for b in range(4)]
def reference(x, gr, w, w2, sn, nb, il):
    G = []
    for r in range(N):
        arrived = mx_ref.quantize(np.concatenate([cols(x[s], entries(sn[s])[r * CAPP:(r + 1) * CAPP]) for s in range(N)], axis=1))
        e = entries(nb[r])
        z = [mx_ref.matmul(W, arrived)[:, e].reshape(128, T, 4) + np.float32(0.0) for W in four(w[r])]
        win = np.stack([v.argmax(axis=2) for v in z], axis=2)
        g = gr[r].reshape(128, T, 4); back = np.zeros((128, N * CAPP, 4), BF)
        for k in range(4): back[:, e[k::4]] = np.where(win == k, g, np.zeros_like(g))
        G.append(back)
    y = np.zeros((N, 128, 4 * T), np.float32)
    for s in range(N):
        q = mx_ref.quantize(np.concatenate([G[r][:, s * CAPP:(s + 1) * CAPP].reshape(128, -1) for r in range(N)], axis=1))
        e = entries(il[s])
        for b, V in enumerate(four(w2[s])):
            u = mx_ref.matmul(V, q); t = np.zeros((128, T), np.float32)
            for i in range(F):
                k = e[i::F]; has = k >= 0
                t[:, has] += u[:, k[has]]
            y[s][:, T * b:T * b + T] = t
    return {"y": y}

from concourse.bass import DstId, RemoteDMATransfer
from concourse.mybir import dt, AluOpType, ActivationFunctionType

NR, NODES, CAPP, F = 8, 128, 80, 8
SLOTS = NR * CAPP
PAD = 8
BIG = 1e29
POS = (1, 3, 7, 5)

SCRATCH = {
    "xs": ("sbuf", [128, 4 * NODES], "bfloat16"),
    "grs": ("sbuf", [128, 4 * NODES], "bfloat16"),
    "ws": ("sbuf", [128, 2048], "bfloat16"),
    "ws2": ("sbuf", [128, 2048], "bfloat16"),
    "snt": ("sbuf", [128, SLOTS // 16], "int32"),
    "nbt": ("sbuf", [128, 4 * NODES // 16], "int32"),
    "ilt": ("sbuf", [128, F * NODES // 16], "int32"),
    "xg": ("sbuf", [128, 4 * SLOTS], "bfloat16"),
    "xq": ("sbuf", [128, SLOTS], "float8_e4m3fn_x4"),
    "xp": ("sbuf", [128, SLOTS], "uint8"),
    "wq": ("sbuf", [128, 512], "float8_e4m3fn_x4"),
    "wp": ("sbuf", [128, 512], "uint8"),
    "vq": ("sbuf", [128, 512], "float8_e4m3fn_x4"),
    "vp": ("sbuf", [128, 512], "uint8"),
    "landq": ("sbuf", [128, SLOTS], "float8_e4m3fn_x4"),
    "landp": ("sbuf", [128, SLOTS], "uint8"),
    "backq": ("sbuf", [128, SLOTS], "float8_e4m3fn_x4"),
    "backp": ("sbuf", [128, SLOTS], "uint8"),
    "gs": ("sbuf", [128, 4 * SLOTS], "bfloat16"),
    "gq": ("sbuf", [128, SLOTS], "float8_e4m3fn_x4"),
    "gp": ("sbuf", [128, SLOTS], "uint8"),
    "ps": ("psum", [128, 4096], "float32"),
    "nbl": ("sbuf", [128, 32], "uint16"),
    "nbm": ("sbuf", [128, 32], "int32"),
    "nbs": ("sbuf", [128, 32], "int32"),
    "scl": ("sbuf", [128, 32], "uint16"),
    "pix": ("sbuf", [128, 1], "int32"),
    "pib": ("sbuf", [128, 1], "int32"),
    "sh": ("sbuf", [128, 1], "float32"),
    "vals": ("sbuf", [128, 512], "float32"),
    "win": ("sbuf", [128, 2 * SLOTS], "float32"),
    "wint": ("sbuf", [128, 2 * SLOTS], "float32"),
    "invf": ("sbuf", [128, 40], "float32"),
    "inv": ("sbuf", [128, 40], "uint16"),
    "ill": ("sbuf", [128, 64], "uint16"),
    "mpat": ("sbuf", [128, 512], "float32"),
    "spat": ("sbuf", [128, 512], "float32"),
    "yt": ("sbuf", [128, 512], "float32"),
}
for _i in range(4):
    SCRATCH["off%d" % _i] = ("sbuf", [128, 40], "uint16")
    SCRATCH["z%d" % _i] = ("sbuf", [128, SLOTS], "float32")
    SCRATCH["zg%d" % _i] = ("sbuf", [128, 512], "float32")
    SCRATCH["pm%d" % _i] = ("sbuf", [128, 512], "float32")
    SCRATCH["grx%d" % _i] = ("sbuf", [128, 1024], "bfloat16")
    SCRATCH["tb%d" % _i] = ("sbuf", [128, 1024], "bfloat16")
    SCRATCH["u%d" % _i] = ("sbuf", [128, PAD + SLOTS], "float32")
for _i in range(2):
    SCRATCH["msk%d" % _i] = ("sbuf", [128, 1024], "bfloat16")
for _i in range(8):
    SCRATCH["ug%d" % _i] = ("sbuf", [128, 512], "float32")
    SCRATCH["us%d" % _i] = ("sbuf", [128, 512], "float32")

SEMAPHORES = ["sv", "ss", "st", "sg", "dsn", "dx", "dw", "dnb", "dgr", "dw2", "dil", "own1", "own2", "dy",
              "aO", "aH", "bO", "bH", "ls"]


def rank_program(g, core, T, topo):
    rank = T.rank_of(core)
    if rank is None:
        return
    A, COPY = AluOpType, ActivationFunctionType.Copy
    V, S, P, Y = g.vector, g.scalar, g.tensor, g.sync
    queue = {"v": V, "s": S, "t": P, "g": g, "y": Y}
    sem_of = {"v": "sv", "s": "ss", "t": "st", "g": "sg"}
    count = {"v": 0, "s": 0, "t": 0, "g": 0}
    seen = {}

    def done(e, ins):
        ins.then_inc(T.sem[sem_of[e]], 1)
        count[e] += 1
        return (sem_of[e], count[e])

    def need(e, *tokens):
        for name, val in tokens:
            if seen.get((e, name), 0) < val:
                queue[e].wait_ge(T.sem[name], val)
                seen[(e, name)] = val

    cores = list(T.cores)
    other = [d for d in range(NR) if topo.host(cores[d]) != topo.host(core)]
    here = [d for d in range(NR) if topo.host(cores[d]) == topo.host(core)]
    o0, h0 = other[0] * CAPP, here[0] * CAPP
    half = len(other) * CAPP
    engines = {}
    for i, d in enumerate(other):
        e = topo.engines(core, cores[d])
        per = len(e) // len(other)
        engines[d] = e[i * per:(i + 1) * per]
    chip_peer = [d for d in here if d != rank and cores[d] in topo.cores_of(core)]
    mates = [d for d in here if d != rank and d not in chip_peer]
    off = topo.engines(core, cores[mates[0]])
    per = len(off) // len(mates)
    for i, d in enumerate(mates):
        engines[d] = off[i * per:(i + 1) * per]
    for d in chip_peer:
        engines[d] = [e for e in topo.engines(core, cores[d]) if e not in off][:per]
    near = chip_peer + mates
    inc_o = 2 * sum(len(engines[d]) for d in other)
    inc_h = 2 * sum(len(engines[d]) for d in near)

    def send(dests, sq, sp, dq, dp, sem):
        for src, dst, codes in ((sq, dq, True), (sp, dp, False)):
            tr = []
            for d in dests:
                rid, pid = topo.addr(cores[d], core)
                a = T[src][:, d * CAPP:(d + 1) * CAPP]
                b = T[dst][:, rank * CAPP:(rank + 1) * CAPP]
                if codes:
                    a, b = a.bitcast(dt.uint8), b.bitcast(dt.uint8)
                tr.append(RemoteDMATransfer(dst_ids=[DstId(rid=rid, pnc=pid)],
                                            dma_engine_mask=sum(1 << e for e in engines[d]),
                                            remote_sem=T.sem[sem], src=a, dst=b))
            g.remote_dma_fused(tr, local_sem=T.sem.ls)

    def keep(sq, sp, dq, dp, sem):
        a, b = rank * CAPP, (rank + 1) * CAPP
        Y.dma_start(out=T[dq][:, a:b].bitcast(dt.uint8), in_=T[sq][:, a:b].bitcast(dt.uint8)).then_inc(T.sem[sem], 16)
        Y.dma_start(out=T[dp][:, a:b], in_=T[sp][:, a:b]).then_inc(T.sem[sem], 16)

    Y.dma_start(out=T.xs[:], in_=T.x[:]).then_inc(T.sem.dx, 16)
    for k in range(4):
        S.dma_start(out=T.snt[16 * k:16 * k + 16, :], in_=T.sn[:, :]).then_inc(T.sem.dsn, 16)
    for k in range(4, 8):
        Y.dma_start(out=T.snt[16 * k:16 * k + 16, :], in_=T.sn[:, :]).then_inc(T.sem.dsn, 16)
    S.dma_start(out=T.ws[:], in_=T.w[:]).then_inc(T.sem.dw, 16)
    for k in range(8):
        Y.dma_start(out=T.nbt[16 * k:16 * k + 16, :], in_=T.nb[:, :]).then_inc(T.sem.dnb, 16)
    Y.dma_start(out=T.grs[:], in_=T.gr[:]).then_inc(T.sem.dgr, 16)
    Y.dma_start(out=T.ws2[:], in_=T.w2[:]).then_inc(T.sem.dw2, 16)
    for k in range(8):
        Y.dma_start(out=T.ilt[16 * k:16 * k + 16, :], in_=T.il[:, :]).then_inc(T.sem.dil, 16)

    pix = done("g", g.iota(T.pix[:], [[0, 1]], 0, 1))
    for k in range(4):
        vals = done("g", g.iota(T.vals[:, k:512:4], [[8, 128]], POS[k], 0, allow_small_or_imprecise_dtypes=True))
    mk = [None, None]
    mk[0] = done("g", g.iota(T.msk0[:, 0:1024:2], [[0, 256], [-1, 2]], 0, 0, allow_small_or_imprecise_dtypes=True))

    t0 = done("v", V.memset(T.mpat[:], BIG))
    grz = [None] * 4
    for b in (2, 3):
        need("s", t0)
        grz[b] = done("s", S.activation(T["grx%d" % b][:, 1:1024:2], T.mpat[:], COPY, scale=0.0))
    win = done("v", V.memset(T.win[:], 0.0))
    for b in (0, 1):
        grz[b] = done("v", V.memset(T["grx%d" % b][:, 1:1024:2], 0.0))
    need("v", t0, *[grz[b] for b in (2, 3)])
    mpat = done("v", V.memset(T.mpat[:, 0:512:4], -BIG))

    need("v", ("dsn", 128))
    offs = {}
    for t in (2, 0, 1, 3):
        offs[t] = done("v", V.tensor_scalar(T["off%d" % t][:], T.snt[:], 4.0, float(t), A.mult, A.add))
    for e in ("v", "s"):
        need(e, ("dx", 16))
    n16 = half // 16

    def gather_x(a):
        toks = []
        for e, t in (("v", 0), ("s", 2), ("v", 1), ("s", 3)):
            need(e, offs[t])
            src = T.xs[:, :].indirect(T["off%d" % t][:, a // 16:a // 16 + n16])
            dst = T.xg[:, 4 * a + t:4 * (a + half):4]
            toks.append(done(e, V.tensor_copy(dst, src) if e == "v" else S.activation(dst, src, COPY)))
        return toks

    def quantise(q, p, t, a, n):
        return done("v", V.quantize_mx(T[q][:, a:a + n], T[p][:, a:a + n], T[t][:, 4 * a:4 * (a + n)]))

    need("v", *gather_x(o0))
    tok = quantise("xq", "xp", "xg", o0, half)
    need("g", tok)
    send(other, "xq", "xp", "landq", "landp", "aO")
    need("v", *gather_x(h0))
    tok = quantise("xq", "xp", "xg", h0, half)
    need("g", tok)
    send(near, "xq", "xp", "landq", "landp", "aH")
    need("y", tok)
    keep("xq", "xp", "landq", "landp", "own1")
    mk[1] = done("g", g.iota(T.msk1[:, 0:1024:2], [[0, 256], [-1, 2]], 0, 0, allow_small_or_imprecise_dtypes=True))

    need("v", ("dw", 16))
    wq = quantise("wq", "wp", "ws", 0, 512)
    need("v", ("dnb", 128), pix)
    a1 = done("v", V.tensor_scalar(T.pib[:], T.pix[:], 16, None, A.bitwise_and))
    a2 = done("v", V.tensor_scalar(T.nbm[:], T.nbt[:], 1008, None, A.bitwise_and))
    nbl = done("v", V.tensor_copy(T.nbl[:], T.nbt[:]))
    need("v", a1)
    a3 = done("v", V.tensor_copy(T.sh[:], T.pib[:]))
    need("v", a2)
    a4 = done("v", V.tensor_tensor(T.nbs[:], T.nbm[:], T.nbt[:], A.add))
    need("v", a3, a4)
    a5 = done("v", V.tensor_scalar(T.scl[:], T.nbs[:], T.sh[:], None, A.add))
    need("v", a5, vals, win)
    a6 = done("v", V.tensor_copy(T.win[:].indirect(T.scl[:]), T.vals[:]))
    need("v", a6)
    a7 = done("v", V.transpose(T.wint[:], T.win[:]))
    need("v", a7)
    a8 = done("v", V.tensor_tensor(T.invf[:], T.wint[:, 0:1280:32], T.wint[:, 16:1280:32], A.add))
    need("v", a8)
    inv = done("v", V.tensor_copy(T.inv[:], T.invf[:]))

    need("s", ("dgr", 16))
    grx = [None] * 4
    for b in range(4):
        for k in range(4):
            grx[b] = done("s", S.activation(T["grx%d" % b][:, 2 * k:1024:8], T.grs[:, b:512:4], COPY))

    def products(stat, plane, rq, rp, a, bank, free):
        toks = []
        for b in range(4):
            need("t", *free[b])
            toks.append(done("t", P.matmul_mx(T.ps[:, 512 * (bank + b):512 * (bank + b) + half],
                                              T[stat][:, 128 * b:128 * b + 128], T[plane][:, 128 * b:128 * b + 128],
                                              T[rq][:, a:a + half], T[rp][:, a:a + half], True, True)))
        return toks

    def unload(e, name, b, a, shift, bank, tok):
        need(e, tok)
        dst = T["%s%d" % (name, b)][:, shift + a:shift + a + half]
        src = T.ps[:, 512 * (bank + b):512 * (bank + b) + half]
        return done(e, V.tensor_copy(dst, src) if e == "v" else S.activation(dst, src, COPY))

    none = [()] * 4
    need("t", wq, ("aO", inc_o))
    pt = products("wq", "wp", "landq", "landp", o0, 0, none)
    zo = [None] * 4
    for b in range(4):
        zo[b] = unload("s" if b % 2 else "v", "z", b, o0, 0, 0, pt[b])
    need("t", ("aH", inc_h), ("own1", 32))
    pt = products("wq", "wp", "landq", "landp", h0, 4, none)
    zh = [None] * 4
    for b in (0, 1, 2, 3):
        zh[b] = unload("s" if b == 1 else "v", "z", b, h0, 0, 4, pt[b])

    zg, sg = [None] * 4, {}

    def order_z(b):
        need("s", zo[b], zh[b], nbl)
        zg[b] = done("s", S.activation(T["zg%d" % b][:], T["z%d" % b][:].indirect(T.nbl[:]), COPY))

    def slots(e, b, a, n):
        need(e, inv, chain[b])
        dst = T.gs[:, 4 * a + b:4 * (a + n):4]
        src = T["tb%d" % b][:].indirect(T.inv[:, a // 16:(a + n) // 16])
        return done(e, V.tensor_copy(dst, src) if e == "v" else S.activation(dst, src, COPY))

    pm, cm, chain = [None] * 4, [None] * 4, [None] * 4

    def running(b):
        need("v", zg[b], mpat)
        pm[b] = done("v", V.tensor_tensor_scan(T["pm%d" % b][:], T.mpat[:], T["zg%d" % b][:], 0.0, A.min, A.max))

    def compare(b):
        need("v", pm[b], mk[b % 2])
        m, k = T["pm%d" % b], T["msk%d" % (b % 2)]
        cm[b] = done("v", V.tensor_tensor(k[:, 3:1024:8], m[:, 1:512:4], m[:, 3:512:4], A.is_ge))
        done("v", V.tensor_tensor(k[:, 1:1024:8], m[:, 0:512:4], m[:, 3:512:4], A.is_ge))
        done("v", V.tensor_tensor(k[:, 5:1024:8], m[:, 2:512:4], m[:, 3:512:4], A.is_lt))
        need("v", cm[b])
        cm[b] = done("v", V.tensor_scalar(k[:, 7:1024:8], k[:, 3:1024:8], -1.0, 1.0, A.mult, A.add))

    def masked(b):
        need("v", cm[b], grx[b], grz[b])
        chain[b] = done("v", V.tensor_tensor_scan(T["tb%d" % b][:], T["msk%d" % (b % 2)][:], T["grx%d" % b][:], 0.0, A.mult, A.add))

    order_z(0)
    order_z(1)
    running(0)
    compare(0)
    running(1)
    masked(0)
    order_z(2)
    slots0 = slots("s", 0, 0, SLOTS)
    compare(1)
    running(2)
    masked(1)
    order_z(3)
    slots1 = slots("s", 1, 0, SLOTS)
    compare(2)
    running(3)
    masked(2)
    slots2 = slots("s", 2, 0, SLOTS)
    compare(3)
    masked(3)
    q1 = slots("v", 3, o0, half // 2)
    q2 = slots("s", 3, o0 + half // 2, half // 2)
    q3 = slots("s", 3, h0, half)
    need("v", q1, slots0, slots1, slots2, q2)
    tok = quantise("gq", "gp", "gs", o0, half)
    need("g", tok)
    send(other, "gq", "gp", "backq", "backp", "bO")
    need("v", q3)
    tok = quantise("gq", "gp", "gs", h0, half)
    need("g", tok)
    send(near, "gq", "gp", "backq", "backp", "bH")
    need("y", tok)
    keep("gq", "gp", "backq", "backp", "own2")

    need("v", ("dw2", 16))
    vq = quantise("vq", "vp", "ws2", 0, 512)
    need("v", ("dil", 128))
    ill = done("v", V.tensor_scalar(T.ill[:], T.ilt[:], float(PAD), None, A.add))
    zpad = [done("v", V.memset(T["u%d" % b][:, 0:PAD], 0.0)) for b in range(4)]
    c1 = done("v", V.memset(T.spat[:], 1.0))
    need("v", c1)
    spat = done("v", V.memset(T.spat[:, 0:512:8], 0.0))

    need("t", vq, ("bO", inc_o))
    pt = products("vq", "vp", "backq", "backp", o0, 0, [(zo[b],) for b in range(4)])
    uo = [None] * 4
    for b in range(4):
        uo[b] = unload("s" if b % 2 else "v", "u", b, o0, PAD, 0, pt[b])
    need("t", ("bH", inc_h), ("own2", 32))
    pt = products("vq", "vp", "backq", "backp", h0, 4, [(zh[b],) for b in range(4)])
    uh = [None] * 4
    for b in range(4):
        uh[b] = unload("s" if b == 1 else "v", "u", b, h0, PAD, 4, pt[b])

    ug, us, yt = [None] * 8, [None] * 8, [None] * 8

    def take(e, i):
        b, h = i // 2, i % 2
        need(e, uo[b], uh[b], zpad[b], ill)
        src = T["u%d" % b][:].indirect(T.ill[:, 32 * h:32 * h + 32])
        dst = T["ug%d" % i][:]
        ug[i] = done(e, V.tensor_copy(dst, src) if e == "v" else S.activation(dst, src, COPY))

    def add_up(i):
        need("v", ug[i], spat)
        us[i] = done("v", V.tensor_tensor_scan(T["us%d" % i][:], T.spat[:], T["ug%d" % i][:], 0.0, A.mult, A.add))

    def pick(i):
        need("v", us[i])
        yt[i] = done("v", V.tensor_copy(T.yt[:, 64 * i:64 * i + 64], T["us%d" % i][:, 7:512:8]))

    def store(b):
        need("y", yt[2 * b], yt[2 * b + 1])
        Y.dma_start(out=T.y[:, 128 * b:128 * b + 128], in_=T.yt[:, 128 * b:128 * b + 128]).then_inc(T.sem.dy, 16)

    for i in range(7):
        take("s", i)
    add_up(0)
    add_up(1)
    pick(0)
    pick(1)
    add_up(2)
    store(0)
    take("v", 7)
    add_up(3)
    pick(2)
    pick(3)
    store(1)
    add_up(4)
    add_up(5)
    pick(4)
    pick(5)
    store(2)
    add_up(7)
    add_up(6)
    pick(7)
    pick(6)
    store(3)

    Y.wait_ge(T.sem.dy, 64)
    need("g", ("sv", count["v"]), ("ss", count["s"]), ("st", count["t"]), ("sg", count["g"]))
    g.wait_ge(T.sem.ls, 2 * (inc_o + inc_h))
